import numpy as np
import ml_dtypes


def mxq(x, axis, fmt="e4m3"):
    dtype, down = {"e4m3": (ml_dtypes.float8_e4m3fn, 7), "e5m2": (ml_dtypes.float8_e5m2, 14)}[fmt]
    v = np.moveaxis(np.asarray(x, np.float32).astype(ml_dtypes.bfloat16).astype(np.float64), axis, -1)
    blocks = v.reshape(v.shape[:-1] + (-1, 32))
    amax = np.abs(blocks).max(-1, keepdims=True)
    byte = np.maximum(np.where(amax > 0, np.frexp(amax)[1] - 1 + 127, 0) - down, 1)
    scale = np.exp2(byte - 127.0)
    codes = (blocks / scale).astype(np.float32).astype(dtype).astype(np.float64)
    return np.moveaxis((codes * scale).reshape(v.shape), -1, axis)


WIDE = False


def mx_kscale(k):
    if not WIDE:
        return np.ones(k)
    levels = np.array([10, -10, 5, -5, 0])
    if k % 512:
        return np.exp2(np.random.permutation(np.resize(levels, k // 32))).repeat(32)
    a = np.empty((k // 512, 16))
    for p in range(k // 512):
        a[p, :8] = np.random.permutation(np.resize(levels, 8))
        for g in range(8):
            far = levels[np.abs(levels - a[p, g]) >= 10]
            a[p, g + 8] = far[np.random.randint(len(far))]
    return np.exp2(a.ravel()).repeat(32)


def f64(x):
    return np.asarray(x).astype(np.float64)


def striped(idx):
    return np.tile(np.asarray(idx).reshape(-1, 16).T, (8, 1)).astype(np.uint16)


def unstriped(offs):
    return offs[:16].T.reshape(-1).astype(np.int64)


E2M1 = np.array([0.0, 0.5, 1.0, 1.5, 2.0, 3.0, 4.0, 6.0, -0.0, -0.5, -1.0, -1.5, -2.0, -3.0, -4.0, -6.0])


def pack_weight(w, fmt):
    k, n = w.shape
    w = f64(np.asarray(w, np.float32).astype(ml_dtypes.bfloat16)).reshape(k // 32, 32, n)
    amax = np.abs(w).max(1)
    if fmt == "e4m3":
        byte = np.frexp(amax)[1] - 1 + 127 - 7
    else:
        mant, ex = np.frexp(amax / 6.0)
        byte = np.where(mant > 0.5, ex, ex - 1) + 127
    byte = np.clip(np.where(amax > 0, byte, 1), 1, 254)
    scaled = (w * np.exp2(127.0 - byte)[:, None, :]).reshape(k, n).astype(np.float32)
    by_word = np.ascontiguousarray(scaled.reshape(k // 512, 128, 4, n).transpose(0, 1, 3, 2))
    if fmt == "e4m3":
        words = by_word.astype(ml_dtypes.float8_e4m3fn).view(np.uint8)
    else:
        c = by_word.astype(ml_dtypes.float4_e2m1fn).view(np.uint8) & 0xF
        words = (c[..., 0::2] | (c[..., 1::2] << 4)).reshape(k // 512, 128, 2 * n)
    return np.ascontiguousarray(words), np.ascontiguousarray(byte.astype(np.uint8).reshape(k // 512, 16, n))


def unpack_weight(words, scales, fmt):
    g, _, n = scales.shape
    words = np.ascontiguousarray(words).reshape(g, 128, n, -1)
    if fmt == "e4m3":
        vals = words.view(ml_dtypes.float8_e4m3fn).astype(np.float64)
    else:
        nib = np.empty((g, 128, n, 4), np.uint8)
        nib[..., 0::2] = words & 0xF
        nib[..., 1::2] = words >> 4
        vals = E2M1[nib]
    vals = vals * np.repeat(np.exp2(scales.astype(np.float64) - 127.0), 8, axis=1)[..., None]
    return vals.transpose(0, 1, 3, 2).reshape(g * 512, n)


D, T, I, Q, E, U, M = 512, 2048, 512, 256, 512, 1024, 1024


def setup_inputs():
    n = np.random.standard_normal
    idx = np.random.permutation(T)[:I]
    idx2 = np.random.permutation(U)[:I]
    idx3 = np.random.permutation(M)[:Q]
    fd = mx_kscale(D)
    fi = mx_kscale(I)
    ti = np.ones(T)
    ti[idx] = fi
    keysp = pack_weight(n((D, T)) / fd[:, None], "e4m3")
    return {
        "query": (n((D, Q)) * 0.7 / np.sqrt(D) * fd[:, None]).astype(np.float32),
        "query2": (n((D, Q)) * 0.7 / np.sqrt(D) * fd[:, None]).astype(np.float32),
        "keys_words": keysp[0],
        "keys_scales": keysp[1],
        "notes": (n((D, U)) / fd[:, None]).astype(np.float32),
        "os": (np.random.uniform(0.02, 0.08, (1, I)) * fi).astype(np.float32),
        "vals": (n((E, T)) / ti).astype(np.float32),
        "member": (n((E, M))).astype(np.float32),
        "offs": striped(idx),
        "offs2": striped(idx2),
        "offs3": striped(idx3),
    }


def reference(query, query2, keys_words, keys_scales, notes, os, vals, member, offs, offs2, offs3):
    idx = unstriped(offs)
    idx2 = unstriped(offs2)
    idx3 = unstriped(offs3)
    keysu = unpack_weight(keys_words, keys_scales, "e4m3")
    queryq = mxq(f64(query), 0, "e4m3")
    keysidxg = keysu[:, idx]
    query2q = mxq(f64(query2), 0, "e4m3")
    notesidx2q = mxq(f64(notes)[:, idx2], 0, "e4m3")
    s = queryq.T @ keysidxg + query2q.T @ notesidx2q
    w = np.maximum(s, 0.0)
    wo1 = w * f64(os)
    wt1 = wo1.T
    vt1 = f64(vals)[:, idx].T
    vt1q = mxq(vt1, 0, "e4m3")
    wt1q = mxq(wt1, 0, "e4m3")
    o = vt1q.T @ wt1q
    y = np.abs(o - f64(member)[:, idx3])
    return y

@@ -1,0 +1,184 @@
+from contextlib import ExitStack
+
+import concourse.mybir as mybir
+from concourse.masks import make_identity
+
+D, T, I, Q, E, U, M = 512, 2048, 512, 256, 512, 1024, 1024
+FLOPS = 2 * (2 * D * I * Q + I * E * Q)
+
+F32 = mybir.dt.float32
+BF16 = mybir.dt.bfloat16
+I32 = mybir.dt.int32
+U32 = mybir.dt.uint32
+U16 = mybir.dt.uint16
+U8 = mybir.dt.uint8
+FP8X4 = mybir.dt.float8_e4m3fn_x4
+ALU = mybir.AluOpType
+ACT = mybir.ActivationFunctionType
+
+P = 128
+PACK = 4
+
+
+def tile_attend_twosources_distanceout_lean_kernel(
+    tc, query, query2, keys_words, keys_scales, notes, slot_factor, vals, member, offs, offs2, offs3, out
+):
+    nc = tc.nc
+    with ExitStack() as ctx:
+        lists = ctx.enter_context(tc.tile_pool(name="lists", bufs=1))
+        sb = ctx.enter_context(tc.tile_pool(name="sb", bufs=1))
+        ps = ctx.enter_context(tc.psum_pool(name="ps", bufs=1))
+
+        def quantise(name, grouped, width):
+            codes = sb.tile([P, width], U32, name=name + "_codes", align_bytes=64)
+            scales = sb.tile([P, width], U8, name=name + "_scales", align_bytes=64)
+            nc.vector.quantize_mx(out=codes[:].bitcast(FP8X4), scales=scales[:], in_=grouped)
+            return codes, scales
+
+        def mx(acc, stationary, s_cols, moving, m_cols, start, stop):
+            nc.tensor.matmul_mx(
+                out=acc,
+                lhsT=stationary[0][:, s_cols].bitcast(FP8X4),
+                lhsT_scale=stationary[1][:, s_cols],
+                rhs=moving[0][:, m_cols].bitcast(FP8X4),
+                rhs_scale=moving[1][:, m_cols],
+                start=start,
+                stop=stop,
+            )
+
+        token_list = lists.tile([P, I // 16], U16, name="token_list")
+        note_list = lists.tile([P, I // 16], U16, name="note_list")
+        member_list = lists.tile([P, Q // 16], U16, name="member_list")
+
+        key_bytes = sb.tile([P, T], U8, name="key_bytes")
+        nc.gpsimd.memset(key_bytes[:].bitcast(I32), 0)
+
+        notes_rows = notes.rearrange("(p t) u -> p (t u)", t=PACK)
+        note_pool = [sb.tile([P, 2 * U], F32, name=f"note_pool{h}") for h in range(2)]
+        nc.sync.dma_start(out=note_pool[0][:], in_=notes_rows[:, 0 : 2 * U])
+        nc.sync.dma_start(note_list[:], offs2)
+        nc.sync.dma_start(out=note_pool[1][:], in_=notes_rows[:, 2 * U : 4 * U])
+        nc.sync.dma_start(token_list[:], offs)
+        for quad in range(4):
+            nc.sync.dma_start(
+                out=key_bytes[32 * quad : 32 * quad + 4, :].bitcast(I32),
+                in_=keys_scales[0, 4 * quad : 4 * quad + 4, :].bitcast(I32),
+            )
+        key_words = sb.tile([P, T], U32, name="key_words")
+        nc.sync.dma_start(
+            out=key_words[:].bitcast(I32), in_=keys_words[0].rearrange("p n t -> p (n t)").bitcast(I32)
+        )
+        q_raw = []
+        for n, src in enumerate((query, query2)):
+            raw = sb.tile([P, PACK, Q], F32, name=f"q_raw{n}")
+            nc.sync.dma_start(out=raw[:], in_=src.rearrange("(p t) q -> p t q", t=PACK))
+            q_raw.append(raw)
+        factor = sb.tile([P, PACK], F32, name="factor")
+        nc.sync.dma_start(out=factor[:], in_=slot_factor[0].rearrange("(p r) -> p r", r=PACK))
+        val_pool = [sb.tile([P, T], F32, name=f"val_pool{j}") for j in range(E // P)]
+        for j in range(E // P):
+            nc.sync.dma_start(out=val_pool[j][:], in_=vals[j * P : (j + 1) * P, :])
+        nc.sync.dma_start(member_list[:], offs3)
+        member_pool = [sb.tile([P, M], F32, name=f"member_pool{j}") for j in range(E // P)]
+        for j in range(E // P):
+            nc.sync.dma_start(out=member_pool[j][:], in_=member[j * P : (j + 1) * P, :])
+
+        identity = sb.tile([P, P], F32, name="identity")
+        make_identity(nc, identity[:])
+
+        picked_notes = sb.tile([P, PACK, I], F32, name="picked_notes")
+        for h in range(2):
+            nc.scalar.activation(picked_notes[:, 2 * h, :], note_pool[h][:].indirect(note_list[:]), ACT.Copy)
+            nc.vector.tensor_copy(picked_notes[:, 2 * h + 1, :], note_pool[h][:, U : 2 * U].indirect(note_list[:]))
+        key_scales_dealt = sb.tile([P, I], U8, name="key_scales_dealt", align_bytes=64)
+        nc.vector.tensor_copy(
+            key_scales_dealt[:].rearrange("p (r s) -> p s r", r=PACK), key_bytes[:].indirect(token_list[:])
+        )
+        notes_grouped = sb.tile([P, I * PACK], BF16, name="notes_grouped", align_bytes=64)
+        nc.vector.tensor_copy(
+            notes_grouped[:].rearrange("p (r s t) -> p s t r", r=PACK, t=PACK),
+            picked_notes[:].rearrange("p t (s r) -> p s t r", r=PACK),
+        )
+        key_words_dealt = sb.tile([P, I], U32, name="key_words_dealt", align_bytes=64)
+        nc.vector.tensor_copy(
+            key_words_dealt[:].rearrange("p (r s) -> p s r", r=PACK), key_words[:].indirect(token_list[:])
+        )
+        keys_mx = (key_words_dealt, key_scales_dealt)
+        notes_mx = quantise("notes", notes_grouped[:], I)
+
+        q_mx = []
+        q_grouped = [sb.tile([P, Q * PACK], BF16, name=f"q_grouped{n}", align_bytes=64) for n in range(2)]
+        nc.vector.tensor_copy(
+            q_grouped[0][:].rearrange("p (c i t) -> p c t i", i=4, t=PACK),
+            q_raw[0][:].rearrange("p t (c i) -> p c t i", i=4),
+        )
+        nc.scalar.copy(
+            q_grouped[1][:].rearrange("p (c i t) -> p c t i", i=4, t=PACK),
+            q_raw[1][:].rearrange("p t (c i) -> p c t i", i=4),
+        )
+        for n in range(2):
+            q_mx.append(quantise(f"q{n}", q_grouped[n][:], Q))
+
+        w_grouped = sb.tile([P, Q, PACK], BF16, name="w_grouped", align_bytes=64)
+        score_banks = [ps.tile([P, PACK, P], F32, name=f"scores{h}") for h in range(Q // P)]
+        for h in range(Q // P):
+            q_cols = slice(h * P, (h + 1) * P)
+            for r in range(PACK):
+                slots = slice(r * P, (r + 1) * P)
+                mx(score_banks[h][:, r, :], keys_mx, slots, q_mx[0], q_cols, True, False)
+                mx(score_banks[h][:, r, :], notes_mx, slots, q_mx[1], q_cols, False, True)
+
+        tiles = range(E // P)
+        picked = [sb.tile([P, I], BF16, name=f"picked_vals{j}") for j in tiles]
+        v_grouped = [sb.tile([P, P * PACK], BF16, name=f"v_grouped{j}", align_bytes=64) for j in tiles]
+        sums = [sb.tile([P, Q], F32, name=f"total{j}") for j in tiles]
+        accs = [ps.tile([P, Q], F32, name=f"acc{j}") for j in tiles]
+
+        def pick_values(j):
+            window = val_pool[j][:].indirect(token_list[:])
+            if j % 2 == 0:
+                nc.scalar.activation(picked[j][:], window, ACT.Copy)
+            else:
+                nc.vector.tensor_copy(picked[j][:], window)
+
+        def turn_values(j):
+            pairs = picked[j][:].bitcast(F32)
+            turned = ps.tile([P, 2, P], F32, name=f"turned{j % 2}")
+            for u in range(2):
+                nc.tensor.transpose(turned[:, u, :], pairs[:, u::2], identity[:])
+            nc.scalar.copy(
+                v_grouped[j][:].bitcast(F32).rearrange("p (e u) -> p e u", u=2), turned[:].rearrange("p u e -> p e u")
+            )
+
+        def add_up(j):
+            v_mx = quantise(f"v{j}", v_grouped[j][:], P)
+            mx(accs[j][:], v_mx, slice(0, P), w_mx, slice(0, Q), True, True)
+            nc.scalar.copy(sums[j][:], accs[j][:])
+
+        def distance(j):
+            diff = sb.tile([P, Q], F32, name=f"diff{j}")
+            nc.vector.tensor_tensor(diff[:], member_pool[j][:].indirect(member_list[:]), sums[j][:], ALU.subtract)
+            dist = sb.tile([P, Q], F32, name=f"dist{j}")
+            nc.scalar.activation(dist[:], diff[:], ACT.Abs)
+            nc.sync.dma_start(out=out[j * P : (j + 1) * P, :], in_=dist[:])
+
+        pick_values(0)
+        for h in range(Q // P):
+            nc.vector.scalar_tensor_tensor(
+                out=w_grouped[:, h * P : (h + 1) * P, :],
+                in0=score_banks[h][:].rearrange("p r q -> p q r"),
+                scalar=0.0,
+                in1=factor[:].unsqueeze(1).to_broadcast([P, P, PACK]),
+                op0=ALU.max,
+                op1=ALU.mult,
+            )
+        turn_values(0)
+        w_mx = quantise("w", w_grouped[:].rearrange("p q r -> p (q r)"), Q)
+        for j in range(1, E // P):
+            pick_values(j)
+            add_up(j - 1)
+            turn_values(j)
+        distance(0)
+        add_up(E // P - 1)
+        for j in range(1, E // P):
+            distance(j)

@@ -51,19 +51,20 @@ def tile_attend_twosources_distanceout_lean_kernel(
         member_list = lists.tile([P, Q // 16], U16, name="member_list")
 
         key_bytes = sb.tile([P, T], U8, name="key_bytes")
-        nc.gpsimd.memset(key_bytes[:].bitcast(I32), 0)
+        nc.vector.memset(key_bytes[:].bitcast(I32), 0)
+        scale_rows = sb.tile([P, T // 4], I32, name="scale_rows")
 
         notes_rows = notes.rearrange("(p t) u -> p (t u)", t=PACK)
         note_pool = [sb.tile([P, 2 * U], F32, name=f"note_pool{h}") for h in range(2)]
         nc.sync.dma_start(out=note_pool[0][:], in_=notes_rows[:, 0 : 2 * U])
         nc.sync.dma_start(note_list[:], offs2)
-        nc.sync.dma_start(out=note_pool[1][:], in_=notes_rows[:, 2 * U : 4 * U])
         nc.sync.dma_start(token_list[:], offs)
         for quad in range(4):
             nc.sync.dma_start(
-                out=key_bytes[32 * quad : 32 * quad + 4, :].bitcast(I32),
+                out=scale_rows[32 * quad : 32 * quad + 4, :],
                 in_=keys_scales[0, 4 * quad : 4 * quad + 4, :].bitcast(I32),
             )
+        nc.sync.dma_start(out=note_pool[1][:], in_=notes_rows[:, 2 * U : 4 * U])
         key_words = sb.tile([P, T], U32, name="key_words")
         nc.sync.dma_start(
             out=key_words[:].bitcast(I32), in_=keys_words[0].rearrange("p n t -> p (n t)").bitcast(I32)
@@ -75,7 +76,7 @@ def tile_attend_twosources_distanceout_lean_kernel(
             q_raw.append(raw)
         factor = sb.tile([P, PACK], F32, name="factor")
         nc.sync.dma_start(out=factor[:], in_=slot_factor[0].rearrange("(p r) -> p r", r=PACK))
-        val_pool = [sb.tile([P, T], F32, name=f"val_pool{j}") for j in range(E // P)]
+        val_pool = [sb.tile([P, T], F32, name=f"val_pool{j}", tag=f"val_pool{j}") for j in range(E // P)]
         for j in range(E // P):
             nc.sync.dma_start(out=val_pool[j][:], in_=vals[j * P : (j + 1) * P, :])
         nc.sync.dma_start(member_list[:], offs3)
@@ -87,13 +88,21 @@ def tile_attend_twosources_distanceout_lean_kernel(
         make_identity(nc, identity[:])
 
         picked_notes = sb.tile([P, PACK, I], F32, name="picked_notes")
-        for h in range(2):
-            nc.scalar.activation(picked_notes[:, 2 * h, :], note_pool[h][:].indirect(note_list[:]), ACT.Copy)
-            nc.vector.tensor_copy(picked_notes[:, 2 * h + 1, :], note_pool[h][:, U : 2 * U].indirect(note_list[:]))
+        for t in range(PACK):
+            window = note_pool[t // 2][:, (t % 2) * U : (t % 2 + 1) * U].indirect(note_list[:])
+            if t == 1:
+                nc.vector.tensor_copy(picked_notes[:, t, :], window)
+            else:
+                nc.scalar.activation(picked_notes[:, t, :], window, ACT.Copy)
+        for quad in range(4):
+            live = slice(32 * quad, 32 * quad + 4)
+            nc.vector.tensor_copy(key_bytes[live, :].bitcast(I32), scale_rows[live, :])
+
         key_scales_dealt = sb.tile([P, I], U8, name="key_scales_dealt", align_bytes=64)
         nc.vector.tensor_copy(
             key_scales_dealt[:].rearrange("p (r s) -> p s r", r=PACK), key_bytes[:].indirect(token_list[:])
         )
+
         notes_grouped = sb.tile([P, I * PACK], BF16, name="notes_grouped", align_bytes=64)
         nc.vector.tensor_copy(
             notes_grouped[:].rearrange("p (r s t) -> p s t r", r=PACK, t=PACK),
@@ -108,7 +117,7 @@ def tile_attend_twosources_distanceout_lean_kernel(
 
         q_mx = []
         q_grouped = [sb.tile([P, Q * PACK], BF16, name=f"q_grouped{n}", align_bytes=64) for n in range(2)]
-        nc.vector.tensor_copy(
+        nc.scalar.copy(
             q_grouped[0][:].rearrange("p (c i t) -> p c t i", i=4, t=PACK),
             q_raw[0][:].rearrange("p t (c i) -> p c t i", i=4),
         )
@@ -131,28 +140,30 @@ def tile_attend_twosources_distanceout_lean_kernel(
         tiles = range(E // P)
         picked = [sb.tile([P, I], BF16, name=f"picked_vals{j}") for j in tiles]
         v_grouped = [sb.tile([P, P * PACK], BF16, name=f"v_grouped{j}", align_bytes=64) for j in tiles]
-        sums = [sb.tile([P, Q], F32, name=f"total{j}") for j in tiles]
+        sums = {}
         accs = [ps.tile([P, Q], F32, name=f"acc{j}") for j in tiles]
 
         def pick_values(j):
-            window = val_pool[j][:].indirect(token_list[:])
-            if j % 2 == 0:
-                nc.scalar.activation(picked[j][:], window, ACT.Copy)
+            if j < 2:
+                nc.scalar.activation(picked[j][:], val_pool[j][:].indirect(token_list[:]), ACT.Copy)
             else:
-                nc.vector.tensor_copy(picked[j][:], window)
+                half, cols = I // 2, I // 32
+                nc.scalar.activation(picked[j][:, :half], val_pool[j][:].indirect(token_list[:, :cols]), ACT.Copy)
+                nc.vector.tensor_copy(picked[j][:, half:], val_pool[j][:].indirect(token_list[:, cols:]))
 
         def turn_values(j):
             pairs = picked[j][:].bitcast(F32)
             turned = ps.tile([P, 2, P], F32, name=f"turned{j % 2}")
             for u in range(2):
                 nc.tensor.transpose(turned[:, u, :], pairs[:, u::2], identity[:])
-            nc.scalar.copy(
+            nc.vector.tensor_copy(
                 v_grouped[j][:].bitcast(F32).rearrange("p (e u) -> p e u", u=2), turned[:].rearrange("p u e -> p e u")
             )
 
         def add_up(j):
             v_mx = quantise(f"v{j}", v_grouped[j][:], P)
             mx(accs[j][:], v_mx, slice(0, P), w_mx, slice(0, Q), True, True)
+            sums[j] = sb.tile([P, Q], F32, name=f"total{j}", tag=f"val_pool{j + 1}")
             nc.scalar.copy(sums[j][:], accs[j][:])
 
         def distance(j):

@@ -29,8 +29,8 @@ def tile_attend_twosources_distanceout_lean_kernel(
         sb = ctx.enter_context(tc.tile_pool(name="sb", bufs=1))
         ps = ctx.enter_context(tc.psum_pool(name="ps", bufs=1))
 
-        def quantise(name, grouped, width):
-            codes = sb.tile([P, width], U32, name=name + "_codes", align_bytes=64)
+        def quantise(name, grouped, width, tag=""):
+            codes = sb.tile([P, width], U32, name=name + "_codes", tag=tag, align_bytes=64)
             scales = sb.tile([P, width], U8, name=name + "_scales", align_bytes=64)
             nc.vector.quantize_mx(out=codes[:].bitcast(FP8X4), scales=scales[:], in_=grouped)
             return codes, scales
@@ -65,22 +65,22 @@ def tile_attend_twosources_distanceout_lean_kernel(
                 in_=keys_scales[0, 4 * quad : 4 * quad + 4, :].bitcast(I32),
             )
         nc.sync.dma_start(out=note_pool[1][:], in_=notes_rows[:, 2 * U : 4 * U])
+        q_raw = []
+        for n, src in enumerate((query2, query)):
+            raw = sb.tile([P, PACK, Q], F32, name=f"q_raw{n}")
+            nc.sync.dma_start(out=raw[:], in_=src.rearrange("(p t) q -> p t q", t=PACK))
+            q_raw.append(raw)
         key_words = sb.tile([P, T], U32, name="key_words")
         nc.sync.dma_start(
             out=key_words[:].bitcast(I32), in_=keys_words[0].rearrange("p n t -> p (n t)").bitcast(I32)
         )
-        q_raw = []
-        for n, src in enumerate((query, query2)):
-            raw = sb.tile([P, PACK, Q], F32, name=f"q_raw{n}")
-            nc.sync.dma_start(out=raw[:], in_=src.rearrange("(p t) q -> p t q", t=PACK))
-            q_raw.append(raw)
         factor = sb.tile([P, PACK], F32, name="factor")
         nc.sync.dma_start(out=factor[:], in_=slot_factor[0].rearrange("(p r) -> p r", r=PACK))
-        val_pool = [sb.tile([P, T], F32, name=f"val_pool{j}", tag=f"val_pool{j}") for j in range(E // P)]
+        val_pool = [sb.tile([P, T], F32, name=f"val_pool{j}", tag=f"val_pool{j}", align_bytes=64) for j in range(E // P)]
         for j in range(E // P):
             nc.sync.dma_start(out=val_pool[j][:], in_=vals[j * P : (j + 1) * P, :])
         nc.sync.dma_start(member_list[:], offs3)
-        member_pool = [sb.tile([P, M], F32, name=f"member_pool{j}") for j in range(E // P)]
+        member_pool = [sb.tile([P, M], F32, name=f"member_pool{j}", tag=f"member_pool{j}", align_bytes=64) for j in range(E // P)]
         for j in range(E // P):
             nc.sync.dma_start(out=member_pool[j][:], in_=member[j * P : (j + 1) * P, :])
 
@@ -90,7 +90,7 @@ def tile_attend_twosources_distanceout_lean_kernel(
         picked_notes = sb.tile([P, PACK, I], F32, name="picked_notes")
         for t in range(PACK):
             window = note_pool[t // 2][:, (t % 2) * U : (t % 2 + 1) * U].indirect(note_list[:])
-            if t == 1:
+            if t % 2 == 1:
                 nc.vector.tensor_copy(picked_notes[:, t, :], window)
             else:
                 nc.scalar.activation(picked_notes[:, t, :], window, ACT.Copy)
@@ -108,11 +108,6 @@ def tile_attend_twosources_distanceout_lean_kernel(
             notes_grouped[:].rearrange("p (r s t) -> p s t r", r=PACK, t=PACK),
             picked_notes[:].rearrange("p t (s r) -> p s t r", r=PACK),
         )
-        key_words_dealt = sb.tile([P, I], U32, name="key_words_dealt", align_bytes=64)
-        nc.vector.tensor_copy(
-            key_words_dealt[:].rearrange("p (r s) -> p s r", r=PACK), key_words[:].indirect(token_list[:])
-        )
-        keys_mx = (key_words_dealt, key_scales_dealt)
         notes_mx = quantise("notes", notes_grouped[:], I)
 
         q_mx = []
@@ -128,48 +123,59 @@ def tile_attend_twosources_distanceout_lean_kernel(
         for n in range(2):
             q_mx.append(quantise(f"q{n}", q_grouped[n][:], Q))
 
+        key_words_dealt = sb.tile([P, I], U32, name="key_words_dealt", align_bytes=64)
+        nc.vector.tensor_copy(
+            key_words_dealt[:].rearrange("p (r s) -> p s r", r=PACK), key_words[:].indirect(token_list[:])
+        )
+        keys_mx = (key_words_dealt, key_scales_dealt)
+
         w_grouped = sb.tile([P, Q, PACK], BF16, name="w_grouped", align_bytes=64)
-        score_banks = [ps.tile([P, PACK, P], F32, name=f"scores{h}") for h in range(Q // P)]
-        for h in range(Q // P):
-            q_cols = slice(h * P, (h + 1) * P)
-            for r in range(PACK):
-                slots = slice(r * P, (r + 1) * P)
-                mx(score_banks[h][:, r, :], keys_mx, slots, q_mx[0], q_cols, True, False)
-                mx(score_banks[h][:, r, :], notes_mx, slots, q_mx[1], q_cols, False, True)
+        score_banks = [ps.tile([P, PACK, P], F32, name=f"scores{h}", tag=f"scores{h}") for h in range(Q // P)]
+        for n, source in enumerate((notes_mx, keys_mx)):
+            for h in range(Q // P):
+                for r in range(PACK):
+                    first, last = (n, r) == (0, 0), (n, r) == (1, PACK - 1)
+                    slots, q_cols = slice(r * P, (r + 1) * P), slice(h * P, (h + 1) * P)
+                    mx(score_banks[h][:, r, :], source, slots, q_mx[n], q_cols, first, last)
 
         tiles = range(E // P)
+        last_tile = E // P - 1
         picked = [sb.tile([P, I], BF16, name=f"picked_vals{j}") for j in tiles]
-        v_grouped = [sb.tile([P, P * PACK], BF16, name=f"v_grouped{j}", align_bytes=64) for j in tiles]
-        sums = {}
-        accs = [ps.tile([P, Q], F32, name=f"acc{j}") for j in tiles]
+        v_grouped, v_mx, sums = {}, {}, {}
+        bank_tags = ["scores0", "scores1", "bank2", "bank3", "bank4"]
 
         def pick_values(j):
-            if j < 2:
-                nc.scalar.activation(picked[j][:], val_pool[j][:].indirect(token_list[:]), ACT.Copy)
+            window = val_pool[j][:].indirect(token_list[:])
+            if j == 0:
+                nc.scalar.activation(picked[j][:], window, ACT.Copy)
             else:
-                half, cols = I // 2, I // 32
-                nc.scalar.activation(picked[j][:, :half], val_pool[j][:].indirect(token_list[:, :cols]), ACT.Copy)
-                nc.vector.tensor_copy(picked[j][:, half:], val_pool[j][:].indirect(token_list[:, cols:]))
+                nc.vector.tensor_copy(picked[j][:], window)
 
         def turn_values(j):
             pairs = picked[j][:].bitcast(F32)
-            turned = ps.tile([P, 2, P], F32, name=f"turned{j % 2}")
+            turned = ps.tile([P, 2, P], F32, name=f"turned{j}", tag=bank_tags[j])
             for u in range(2):
                 nc.tensor.transpose(turned[:, u, :], pairs[:, u::2], identity[:])
-            nc.vector.tensor_copy(
+            v_grouped[j] = sb.tile([P, P * PACK], BF16, name=f"v_grouped{j}", tag=f"v_grouped{j}", align_bytes=64)
+            nc.scalar.copy(
                 v_grouped[j][:].bitcast(F32).rearrange("p (e u) -> p e u", u=2), turned[:].rearrange("p u e -> p e u")
             )
 
+        def quantise_values(j):
+            tag = "member_pool0" if j == last_tile else f"val_pool{j + 1}"
+            v_mx[j] = quantise(f"v{j}", v_grouped[j][:], P, tag)
+
         def add_up(j):
-            v_mx = quantise(f"v{j}", v_grouped[j][:], P)
-            mx(accs[j][:], v_mx, slice(0, P), w_mx, slice(0, Q), True, True)
-            sums[j] = sb.tile([P, Q], F32, name=f"total{j}", tag=f"val_pool{j + 1}")
-            nc.scalar.copy(sums[j][:], accs[j][:])
+            acc = ps.tile([P, Q], F32, name=f"acc{j}", tag=bank_tags[j + 1])
+            mx(acc[:], v_mx[j], slice(0, P), w_mx, slice(0, Q), True, True)
+            sums[j] = sb.tile([P, Q], F32, name=f"total{j}")
+            nc.scalar.copy(sums[j][:], acc[:])
 
         def distance(j):
-            diff = sb.tile([P, Q], F32, name=f"diff{j}")
+            tag = f"v_grouped{last_tile}" if j == 1 else ""
+            diff = sb.tile([P, Q], F32, name=f"diff{j}", tag=tag, align_bytes=64)
             nc.vector.tensor_tensor(diff[:], member_pool[j][:].indirect(member_list[:]), sums[j][:], ALU.subtract)
-            dist = sb.tile([P, Q], F32, name=f"dist{j}")
+            dist = sb.tile([P, Q], F32, name=f"dist{j}", tag="member_pool0" if j == 1 else "", align_bytes=64)
             nc.scalar.activation(dist[:], diff[:], ACT.Abs)
             nc.sync.dma_start(out=out[j * P : (j + 1) * P, :], in_=dist[:])
 
@@ -187,9 +193,11 @@ def tile_attend_twosources_distanceout_lean_kernel(
         w_mx = quantise("w", w_grouped[:].rearrange("p q r -> p (q r)"), Q)
         for j in range(1, E // P):
             pick_values(j)
-            add_up(j - 1)
+            quantise_values(j - 1)
             turn_values(j)
+            add_up(j - 1)
         distance(0)
-        add_up(E // P - 1)
+        quantise_values(last_tile)
+        add_up(last_tile)
         for j in range(1, E // P):
             distance(j)

@@ -56,20 +56,18 @@ def tile_attend_twosources_distanceout_lean_kernel(
 
         notes_rows = notes.rearrange("(p t) u -> p (t u)", t=PACK)
         note_pool = [sb.tile([P, 2 * U], F32, name=f"note_pool{h}") for h in range(2)]
-        nc.sync.dma_start(out=note_pool[0][:], in_=notes_rows[:, 0 : 2 * U])
-        nc.sync.dma_start(note_list[:], offs2)
+        q_raw = [sb.tile([P, PACK, Q], F32, name=f"q_raw{n}") for n in range(2)]
+        nc.sync.dma_start(out=q_raw[0][:], in_=query2.rearrange("(p t) q -> p t q", t=PACK))
         nc.sync.dma_start(token_list[:], offs)
         for quad in range(4):
             nc.sync.dma_start(
                 out=scale_rows[32 * quad : 32 * quad + 4, :],
                 in_=keys_scales[0, 4 * quad : 4 * quad + 4, :].bitcast(I32),
             )
+        nc.sync.dma_start(out=note_pool[0][:], in_=notes_rows[:, 0 : 2 * U])
+        nc.sync.dma_start(note_list[:], offs2)
         nc.sync.dma_start(out=note_pool[1][:], in_=notes_rows[:, 2 * U : 4 * U])
-        q_raw = []
-        for n, src in enumerate((query2, query)):
-            raw = sb.tile([P, PACK, Q], F32, name=f"q_raw{n}")
-            nc.sync.dma_start(out=raw[:], in_=src.rearrange("(p t) q -> p t q", t=PACK))
-            q_raw.append(raw)
+        nc.sync.dma_start(out=q_raw[1][:], in_=query.rearrange("(p t) q -> p t q", t=PACK))
         key_words = sb.tile([P, T], U32, name="key_words")
         nc.sync.dma_start(
             out=key_words[:].bitcast(I32), in_=keys_words[0].rearrange("p n t -> p (n t)").bitcast(I32)
@@ -87,13 +85,6 @@ def tile_attend_twosources_distanceout_lean_kernel(
         identity = sb.tile([P, P], F32, name="identity")
         make_identity(nc, identity[:])
 
-        picked_notes = sb.tile([P, PACK, I], F32, name="picked_notes")
-        for t in range(PACK):
-            window = note_pool[t // 2][:, (t % 2) * U : (t % 2 + 1) * U].indirect(note_list[:])
-            if t % 2 == 1:
-                nc.vector.tensor_copy(picked_notes[:, t, :], window)
-            else:
-                nc.scalar.activation(picked_notes[:, t, :], window, ACT.Copy)
         for quad in range(4):
             live = slice(32 * quad, 32 * quad + 4)
             nc.vector.tensor_copy(key_bytes[live, :].bitcast(I32), scale_rows[live, :])
@@ -103,6 +94,13 @@ def tile_attend_twosources_distanceout_lean_kernel(
             key_scales_dealt[:].rearrange("p (r s) -> p s r", r=PACK), key_bytes[:].indirect(token_list[:])
         )
 
+        picked_notes = sb.tile([P, PACK, I], F32, name="picked_notes")
+        for t in range(PACK):
+            window = note_pool[t // 2][:, (t % 2) * U : (t % 2 + 1) * U].indirect(note_list[:])
+            if t % 2 == 1:
+                nc.vector.tensor_copy(picked_notes[:, t, :], window)
+            else:
+                nc.scalar.activation(picked_notes[:, t, :], window, ACT.Copy)
         notes_grouped = sb.tile([P, I * PACK], BF16, name="notes_grouped", align_bytes=64)
         nc.vector.tensor_copy(
             notes_grouped[:].rearrange("p (r s t) -> p s t r", r=PACK, t=PACK),
@@ -146,7 +144,7 @@ def tile_attend_twosources_distanceout_lean_kernel(
 
         def pick_values(j):
             window = val_pool[j][:].indirect(token_list[:])
-            if j == 0:
+            if j < 2:
                 nc.scalar.activation(picked[j][:], window, ACT.Copy)
             else:
                 nc.vector.tensor_copy(picked[j][:], window)
@@ -162,7 +160,7 @@ def tile_attend_twosources_distanceout_lean_kernel(
             )
 
         def quantise_values(j):
-            tag = "member_pool0" if j == last_tile else f"val_pool{j + 1}"
+            tag = ("", "val_pool2", "val_pool3", "member_pool0")[j]
             v_mx[j] = quantise(f"v{j}", v_grouped[j][:], P, tag)
 
         def add_up(j):
@@ -174,10 +172,14 @@ def tile_attend_twosources_distanceout_lean_kernel(
         def distance(j):
             tag = f"v_grouped{last_tile}" if j == 1 else ""
             diff = sb.tile([P, Q], F32, name=f"diff{j}", tag=tag, align_bytes=64)
-            nc.vector.tensor_tensor(diff[:], member_pool[j][:].indirect(member_list[:]), sums[j][:], ALU.subtract)
             dist = sb.tile([P, Q], F32, name=f"dist{j}", tag="member_pool0" if j == 1 else "", align_bytes=64)
-            nc.scalar.activation(dist[:], diff[:], ACT.Abs)
-            nc.sync.dma_start(out=out[j * P : (j + 1) * P, :], in_=dist[:])
+            width = Q // 2 if j == last_tile else Q
+            for q0 in range(0, Q, width):
+                cols = slice(q0, q0 + width)
+                window = member_pool[j][:].indirect(member_list[:, q0 // 16 : (q0 + width) // 16])
+                nc.vector.tensor_tensor(diff[:, cols], window, sums[j][:, cols], ALU.subtract)
+                nc.scalar.activation(dist[:, cols], diff[:, cols], ACT.Abs)
+                nc.sync.dma_start(out=out[j * P : (j + 1) * P, cols], in_=dist[:, cols])
 
         pick_values(0)
         for h in range(Q // P):

@@ -18,6 +18,15 @@ ACT = mybir.ActivationFunctionType
 
 P = 128
 PACK = 4
+QUADRANT = 32
+SCALE_ROWS = 4
+BLOCKS = D // 32
+PER_COLUMN = 16
+RUN = 4
+E_TILES = E // P
+LAST = E_TILES - 1
+SCALAR_PICKS = 2
+ALIGN = 64
 
 
 def tile_attend_twosources_distanceout_lean_kernel(
@@ -30,8 +39,8 @@ def tile_attend_twosources_distanceout_lean_kernel(
         ps = ctx.enter_context(tc.psum_pool(name="ps", bufs=1))
 
         def quantise(name, grouped, width, tag=""):
-            codes = sb.tile([P, width], U32, name=name + "_codes", tag=tag, align_bytes=64)
-            scales = sb.tile([P, width], U8, name=name + "_scales", align_bytes=64)
+            codes = sb.tile([P, width], U32, name=name + "_codes", tag=tag, align_bytes=ALIGN)
+            scales = sb.tile([P, width], U8, name=name + "_scales", align_bytes=ALIGN)
             nc.vector.quantize_mx(out=codes[:].bitcast(FP8X4), scales=scales[:], in_=grouped)
             return codes, scales
 
@@ -46,24 +55,20 @@ def tile_attend_twosources_distanceout_lean_kernel(
                 stop=stop,
             )
 
-        token_list = lists.tile([P, I // 16], U16, name="token_list")
-        note_list = lists.tile([P, I // 16], U16, name="note_list")
-        member_list = lists.tile([P, Q // 16], U16, name="member_list")
+        token_list = lists.tile([P, I // PER_COLUMN], U16, name="token_list")
+        note_list = lists.tile([P, I // PER_COLUMN], U16, name="note_list")
+        member_list = lists.tile([P, Q // PER_COLUMN], U16, name="member_list")
 
         key_bytes = sb.tile([P, T], U8, name="key_bytes")
         nc.vector.memset(key_bytes[:].bitcast(I32), 0)
-        scale_rows = sb.tile([P, T // 4], I32, name="scale_rows")
+        scale_rows = sb.tile([P, T // PACK], I32, name="scale_rows")
 
         notes_rows = notes.rearrange("(p t) u -> p (t u)", t=PACK)
         note_pool = [sb.tile([P, 2 * U], F32, name=f"note_pool{h}") for h in range(2)]
         q_raw = [sb.tile([P, PACK, Q], F32, name=f"q_raw{n}") for n in range(2)]
         nc.sync.dma_start(out=q_raw[0][:], in_=query2.rearrange("(p t) q -> p t q", t=PACK))
         nc.sync.dma_start(token_list[:], offs)
-        for quad in range(4):
-            nc.sync.dma_start(
-                out=scale_rows[32 * quad : 32 * quad + 4, :],
-                in_=keys_scales[0, 4 * quad : 4 * quad + 4, :].bitcast(I32),
-            )
+        nc.sync.dma_start(out=scale_rows[:BLOCKS, :], in_=keys_scales[0].bitcast(I32))
         nc.sync.dma_start(out=note_pool[0][:], in_=notes_rows[:, 0 : 2 * U])
         nc.sync.dma_start(note_list[:], offs2)
         nc.sync.dma_start(out=note_pool[1][:], in_=notes_rows[:, 2 * U : 4 * U])
@@ -74,25 +79,34 @@ def tile_attend_twosources_distanceout_lean_kernel(
         )
         factor = sb.tile([P, PACK], F32, name="factor")
         nc.sync.dma_start(out=factor[:], in_=slot_factor[0].rearrange("(p r) -> p r", r=PACK))
-        val_pool = [sb.tile([P, T], F32, name=f"val_pool{j}", tag=f"val_pool{j}", align_bytes=64) for j in range(E // P)]
-        for j in range(E // P):
+        val_pool = [
+            sb.tile([P, T], F32, name=f"val_pool{j}", tag=f"val_pool{j}", align_bytes=ALIGN) for j in range(E_TILES)
+        ]
+        for j in range(E_TILES):
             nc.sync.dma_start(out=val_pool[j][:], in_=vals[j * P : (j + 1) * P, :])
         nc.sync.dma_start(member_list[:], offs3)
-        member_pool = [sb.tile([P, M], F32, name=f"member_pool{j}", tag=f"member_pool{j}", align_bytes=64) for j in range(E // P)]
-        for j in range(E // P):
+        member_pool = [
+            sb.tile([P, M], F32, name=f"member_pool{j}", tag=f"member_pool{j}", align_bytes=ALIGN)
+            for j in range(E_TILES)
+        ]
+        for j in range(E_TILES):
             nc.sync.dma_start(out=member_pool[j][:], in_=member[j * P : (j + 1) * P, :])
 
         identity = sb.tile([P, P], F32, name="identity")
         make_identity(nc, identity[:])
 
-        for quad in range(4):
-            live = slice(32 * quad, 32 * quad + 4)
-            nc.vector.tensor_copy(key_bytes[live, :].bitcast(I32), scale_rows[live, :])
-
-        key_scales_dealt = sb.tile([P, I], U8, name="key_scales_dealt", align_bytes=64)
+        nc.vector.tensor_copy(key_bytes[:BLOCKS, :].bitcast(I32), scale_rows[:BLOCKS, :])
+        picked_scales = sb.tile([P, I], U8, name="picked_scales")
         nc.vector.tensor_copy(
-            key_scales_dealt[:].rearrange("p (r s) -> p s r", r=PACK), key_bytes[:].indirect(token_list[:])
+            picked_scales[:].rearrange("p (r s) -> p s r", r=PACK), key_bytes[:].indirect(token_list[:])
         )
+        key_scales_dealt = sb.tile([P, I], U8, name="key_scales_dealt", align_bytes=ALIGN)
+        nc.vector.memset(key_scales_dealt[:].bitcast(I32), 0)
+        for quad in range(P // QUADRANT):
+            nc.gpsimd.dma_start(
+                out=key_scales_dealt[QUADRANT * quad : QUADRANT * quad + SCALE_ROWS, :].bitcast(I32),
+                in_=picked_scales[SCALE_ROWS * quad : SCALE_ROWS * (quad + 1), :].bitcast(I32),
+            )
 
         picked_notes = sb.tile([P, PACK, I], F32, name="picked_notes")
         for t in range(PACK):
@@ -101,34 +115,30 @@ def tile_attend_twosources_distanceout_lean_kernel(
                 nc.vector.tensor_copy(picked_notes[:, t, :], window)
             else:
                 nc.scalar.activation(picked_notes[:, t, :], window, ACT.Copy)
-        notes_grouped = sb.tile([P, I * PACK], BF16, name="notes_grouped", align_bytes=64)
+        notes_grouped = sb.tile([P, I * PACK], BF16, name="notes_grouped", align_bytes=ALIGN)
         nc.vector.tensor_copy(
             notes_grouped[:].rearrange("p (r s t) -> p s t r", r=PACK, t=PACK),
             picked_notes[:].rearrange("p t (s r) -> p s t r", r=PACK),
         )
         notes_mx = quantise("notes", notes_grouped[:], I)
 
-        q_mx = []
-        q_grouped = [sb.tile([P, Q * PACK], BF16, name=f"q_grouped{n}", align_bytes=64) for n in range(2)]
-        nc.scalar.copy(
-            q_grouped[0][:].rearrange("p (c i t) -> p c t i", i=4, t=PACK),
-            q_raw[0][:].rearrange("p t (c i) -> p c t i", i=4),
-        )
-        nc.scalar.copy(
-            q_grouped[1][:].rearrange("p (c i t) -> p c t i", i=4, t=PACK),
-            q_raw[1][:].rearrange("p t (c i) -> p c t i", i=4),
-        )
+        q_grouped = [sb.tile([P, Q * PACK], BF16, name=f"q_grouped{n}", align_bytes=ALIGN) for n in range(2)]
         for n in range(2):
-            q_mx.append(quantise(f"q{n}", q_grouped[n][:], Q))
+            nc.scalar.copy(
+                q_grouped[n][:].rearrange("p (c i t) -> p c t i", i=RUN, t=PACK),
+                q_raw[n][:].rearrange("p t (c i) -> p c t i", i=RUN),
+            )
+        q_mx = [quantise(f"q{n}", q_grouped[n][:], Q) for n in range(2)]
 
-        key_words_dealt = sb.tile([P, I], U32, name="key_words_dealt", align_bytes=64)
+        key_words_dealt = sb.tile([P, I], U32, name="key_words_dealt", align_bytes=ALIGN)
         nc.vector.tensor_copy(
             key_words_dealt[:].rearrange("p (r s) -> p s r", r=PACK), key_words[:].indirect(token_list[:])
         )
         keys_mx = (key_words_dealt, key_scales_dealt)
 
-        w_grouped = sb.tile([P, Q, PACK], BF16, name="w_grouped", align_bytes=64)
-        score_banks = [ps.tile([P, PACK, P], F32, name=f"scores{h}", tag=f"scores{h}") for h in range(Q // P)]
+        w_grouped = sb.tile([P, Q, PACK], BF16, name="w_grouped", align_bytes=ALIGN)
+        bank_tags = [f"bank{b}" for b in range(E_TILES + 1)]
+        score_banks = [ps.tile([P, PACK, P], F32, name=f"scores{h}", tag=bank_tags[h]) for h in range(Q // P)]
         for n, source in enumerate((notes_mx, keys_mx)):
             for h in range(Q // P):
                 for r in range(PACK):
@@ -136,48 +146,50 @@ def tile_attend_twosources_distanceout_lean_kernel(
                     slots, q_cols = slice(r * P, (r + 1) * P), slice(h * P, (h + 1) * P)
                     mx(score_banks[h][:, r, :], source, slots, q_mx[n], q_cols, first, last)
 
-        tiles = range(E // P)
-        last_tile = E // P - 1
-        picked = [sb.tile([P, I], BF16, name=f"picked_vals{j}") for j in tiles]
+        picked_vals = [sb.tile([P, I], BF16, name=f"picked_vals{j}") for j in range(E_TILES)]
         v_grouped, v_mx, sums = {}, {}, {}
-        bank_tags = ["scores0", "scores1", "bank2", "bank3", "bank4"]
 
         def pick_values(j):
             window = val_pool[j][:].indirect(token_list[:])
-            if j < 2:
-                nc.scalar.activation(picked[j][:], window, ACT.Copy)
+            if j < SCALAR_PICKS:
+                nc.scalar.activation(picked_vals[j][:], window, ACT.Copy)
             else:
-                nc.vector.tensor_copy(picked[j][:], window)
+                nc.vector.tensor_copy(picked_vals[j][:], window)
 
         def turn_values(j):
-            pairs = picked[j][:].bitcast(F32)
+            pairs = picked_vals[j][:].bitcast(F32)
             turned = ps.tile([P, 2, P], F32, name=f"turned{j}", tag=bank_tags[j])
             for u in range(2):
                 nc.tensor.transpose(turned[:, u, :], pairs[:, u::2], identity[:])
-            v_grouped[j] = sb.tile([P, P * PACK], BF16, name=f"v_grouped{j}", tag=f"v_grouped{j}", align_bytes=64)
+            v_grouped[j] = sb.tile([P, P * PACK], BF16, name=f"v_grouped{j}", tag=f"v_grouped{j}", align_bytes=ALIGN)
             nc.scalar.copy(
                 v_grouped[j][:].bitcast(F32).rearrange("p (e u) -> p e u", u=2), turned[:].rearrange("p u e -> p e u")
             )
 
         def quantise_values(j):
-            tag = ("", "val_pool2", "val_pool3", "member_pool0")[j]
+            if j == LAST:
+                tag = "member_pool0"
+            else:
+                tag = f"val_pool{j + 1}" if j + 1 >= SCALAR_PICKS else ""
             v_mx[j] = quantise(f"v{j}", v_grouped[j][:], P, tag)
 
         def add_up(j):
             acc = ps.tile([P, Q], F32, name=f"acc{j}", tag=bank_tags[j + 1])
             mx(acc[:], v_mx[j], slice(0, P), w_mx, slice(0, Q), True, True)
-            sums[j] = sb.tile([P, Q], F32, name=f"total{j}")
+            sums[j] = sb.tile([P, Q], F32, name=f"sums{j}")
             nc.scalar.copy(sums[j][:], acc[:])
 
         def distance(j):
-            tag = f"v_grouped{last_tile}" if j == 1 else ""
-            diff = sb.tile([P, Q], F32, name=f"diff{j}", tag=tag, align_bytes=64)
-            dist = sb.tile([P, Q], F32, name=f"dist{j}", tag="member_pool0" if j == 1 else "", align_bytes=64)
-            width = Q // 2 if j == last_tile else Q
+            second = j == 1
+            diff = sb.tile([P, Q], F32, name=f"diff{j}", tag=f"v_grouped{LAST}" if second else "", align_bytes=ALIGN)
+            dist = sb.tile([P, Q], F32, name=f"dist{j}", tag="member_pool0" if second else "", align_bytes=ALIGN)
+            width = Q // 2 if j == LAST else Q
             for q0 in range(0, Q, width):
                 cols = slice(q0, q0 + width)
-                window = member_pool[j][:].indirect(member_list[:, q0 // 16 : (q0 + width) // 16])
-                nc.vector.tensor_tensor(diff[:, cols], window, sums[j][:, cols], ALU.subtract)
+                entries = member_list[:, q0 // PER_COLUMN : (q0 + width) // PER_COLUMN]
+                nc.vector.tensor_tensor(
+                    diff[:, cols], member_pool[j][:].indirect(entries), sums[j][:, cols], ALU.subtract
+                )
                 nc.scalar.activation(dist[:, cols], diff[:, cols], ACT.Abs)
                 nc.sync.dma_start(out=out[j * P : (j + 1) * P, cols], in_=dist[:, cols])
 
@@ -193,13 +205,13 @@ def tile_attend_twosources_distanceout_lean_kernel(
             )
         turn_values(0)
         w_mx = quantise("w", w_grouped[:].rearrange("p q r -> p (q r)"), Q)
-        for j in range(1, E // P):
+        for j in range(1, E_TILES):
             pick_values(j)
             quantise_values(j - 1)
             turn_values(j)
             add_up(j - 1)
         distance(0)
-        quantise_values(last_tile)
-        add_up(last_tile)
-        for j in range(1, E // P):
+        quantise_values(LAST)
+        add_up(LAST)
+        for j in range(1, E_TILES):
             distance(j)

from contextlib import ExitStack

import concourse.mybir as mybir
from concourse.masks import make_identity

D, T, I, Q, E, U, M = 512, 2048, 512, 256, 512, 1024, 1024
FLOPS = 2 * (2 * D * I * Q + I * E * Q)

F32 = mybir.dt.float32
BF16 = mybir.dt.bfloat16
I32 = mybir.dt.int32
U32 = mybir.dt.uint32
U16 = mybir.dt.uint16
U8 = mybir.dt.uint8
FP8X4 = mybir.dt.float8_e4m3fn_x4
ALU = mybir.AluOpType
ACT = mybir.ActivationFunctionType

P = 128
PACK = 4
QUADRANT = 32
SCALE_ROWS = 4
BLOCKS = D // 32
PER_COLUMN = 16
RUN = 4
E_TILES = E // P
LAST = E_TILES - 1
SCALAR_PICKS = 2
ALIGN = 64


def tile_attend_twosources_distanceout_lean_kernel(
    tc, query, query2, keys_words, keys_scales, notes, slot_factor, vals, member, offs, offs2, offs3, out
):
    nc = tc.nc
    with ExitStack() as ctx:
        lists = ctx.enter_context(tc.tile_pool(name="lists", bufs=1))
        sb = ctx.enter_context(tc.tile_pool(name="sb", bufs=1))
        ps = ctx.enter_context(tc.psum_pool(name="ps", bufs=1))

        def quantise(name, grouped, width, tag=""):
            codes = sb.tile([P, width], U32, name=name + "_codes", tag=tag, align_bytes=ALIGN)
            scales = sb.tile([P, width], U8, name=name + "_scales", align_bytes=ALIGN)
            nc.vector.quantize_mx(out=codes[:].bitcast(FP8X4), scales=scales[:], in_=grouped)
            return codes, scales

        def mx(acc, stationary, s_cols, moving, m_cols, start, stop):
            nc.tensor.matmul_mx(
                out=acc,
                lhsT=stationary[0][:, s_cols].bitcast(FP8X4),
                lhsT_scale=stationary[1][:, s_cols],
                rhs=moving[0][:, m_cols].bitcast(FP8X4),
                rhs_scale=moving[1][:, m_cols],
                start=start,
                stop=stop,
            )

        token_list = lists.tile([P, I // PER_COLUMN], U16, name="token_list")
        note_list = lists.tile([P, I // PER_COLUMN], U16, name="note_list")
        member_list = lists.tile([P, Q // PER_COLUMN], U16, name="member_list")

        key_bytes = sb.tile([P, T], U8, name="key_bytes")
        nc.vector.memset(key_bytes[:].bitcast(I32), 0)
        scale_rows = sb.tile([P, T // PACK], I32, name="scale_rows")

        notes_rows = notes.rearrange("(p t) u -> p (t u)", t=PACK)
        note_pool = [sb.tile([P, 2 * U], F32, name=f"note_pool{h}") for h in range(2)]
        q_raw = [sb.tile([P, PACK, Q], F32, name=f"q_raw{n}") for n in range(2)]
        nc.sync.dma_start(out=q_raw[0][:], in_=query2.rearrange("(p t) q -> p t q", t=PACK))
        nc.sync.dma_start(token_list[:], offs)
        nc.sync.dma_start(out=scale_rows[:BLOCKS, :], in_=keys_scales[0].bitcast(I32))
        nc.sync.dma_start(out=note_pool[0][:], in_=notes_rows[:, 0 : 2 * U])
        nc.sync.dma_start(note_list[:], offs2)
        nc.sync.dma_start(out=note_pool[1][:], in_=notes_rows[:, 2 * U : 4 * U])
        nc.sync.dma_start(out=q_raw[1][:], in_=query.rearrange("(p t) q -> p t q", t=PACK))
        key_words = sb.tile([P, T], U32, name="key_words")
        nc.sync.dma_start(
            out=key_words[:].bitcast(I32), in_=keys_words[0].rearrange("p n t -> p (n t)").bitcast(I32)
        )
        factor = sb.tile([P, PACK], F32, name="factor")
        nc.sync.dma_start(out=factor[:], in_=slot_factor[0].rearrange("(p r) -> p r", r=PACK))
        val_pool = [
            sb.tile([P, T], F32, name=f"val_pool{j}", tag=f"val_pool{j}", align_bytes=ALIGN) for j in range(E_TILES)
        ]
        for j in range(E_TILES):
            nc.sync.dma_start(out=val_pool[j][:], in_=vals[j * P : (j + 1) * P, :])
        nc.sync.dma_start(member_list[:], offs3)
        member_pool = [
            sb.tile([P, M], F32, name=f"member_pool{j}", tag=f"member_pool{j}", align_bytes=ALIGN)
            for j in range(E_TILES)
        ]
        for j in range(E_TILES):
            nc.sync.dma_start(out=member_pool[j][:], in_=member[j * P : (j + 1) * P, :])

        identity = sb.tile([P, P], F32, name="identity")
        make_identity(nc, identity[:])

        nc.vector.tensor_copy(key_bytes[:BLOCKS, :].bitcast(I32), scale_rows[:BLOCKS, :])
        picked_scales = sb.tile([P, I], U8, name="picked_scales")
        nc.vector.tensor_copy(
            picked_scales[:].rearrange("p (r s) -> p s r", r=PACK), key_bytes[:].indirect(token_list[:])
        )
        key_scales_dealt = sb.tile([P, I], U8, name="key_scales_dealt", align_bytes=ALIGN)
        nc.vector.memset(key_scales_dealt[:].bitcast(I32), 0)
        for quad in range(P // QUADRANT):
            nc.gpsimd.dma_start(
                out=key_scales_dealt[QUADRANT * quad : QUADRANT * quad + SCALE_ROWS, :].bitcast(I32),
                in_=picked_scales[SCALE_ROWS * quad : SCALE_ROWS * (quad + 1), :].bitcast(I32),
            )

        picked_notes = sb.tile([P, PACK, I], F32, name="picked_notes")
        for t in range(PACK):
            window = note_pool[t // 2][:, (t % 2) * U : (t % 2 + 1) * U].indirect(note_list[:])
            if t % 2 == 1:
                nc.vector.tensor_copy(picked_notes[:, t, :], window)
            else:
                nc.scalar.activation(picked_notes[:, t, :], window, ACT.Copy)
        notes_grouped = sb.tile([P, I * PACK], BF16, name="notes_grouped", align_bytes=ALIGN)
        nc.vector.tensor_copy(
            notes_grouped[:].rearrange("p (r s t) -> p s t r", r=PACK, t=PACK),
            picked_notes[:].rearrange("p t (s r) -> p s t r", r=PACK),
        )
        notes_mx = quantise("notes", notes_grouped[:], I)

        q_grouped = [sb.tile([P, Q * PACK], BF16, name=f"q_grouped{n}", align_bytes=ALIGN) for n in range(2)]
        for n in range(2):
            nc.scalar.copy(
                q_grouped[n][:].rearrange("p (c i t) -> p c t i", i=RUN, t=PACK),
                q_raw[n][:].rearrange("p t (c i) -> p c t i", i=RUN),
            )
        q_mx = [quantise(f"q{n}", q_grouped[n][:], Q) for n in range(2)]

        key_words_dealt = sb.tile([P, I], U32, name="key_words_dealt", align_bytes=ALIGN)
        nc.vector.tensor_copy(
            key_words_dealt[:].rearrange("p (r s) -> p s r", r=PACK), key_words[:].indirect(token_list[:])
        )
        keys_mx = (key_words_dealt, key_scales_dealt)

        w_grouped = sb.tile([P, Q, PACK], BF16, name="w_grouped", align_bytes=ALIGN)
        bank_tags = [f"bank{b}" for b in range(E_TILES + 1)]
        score_banks = [ps.tile([P, PACK, P], F32, name=f"scores{h}", tag=bank_tags[h]) for h in range(Q // P)]
        for n, source in enumerate((notes_mx, keys_mx)):
            for h in range(Q // P):
                for r in range(PACK):
                    first, last = (n, r) == (0, 0), (n, r) == (1, PACK - 1)
                    slots, q_cols = slice(r * P, (r + 1) * P), slice(h * P, (h + 1) * P)
                    mx(score_banks[h][:, r, :], source, slots, q_mx[n], q_cols, first, last)

        picked_vals = [sb.tile([P, I], BF16, name=f"picked_vals{j}") for j in range(E_TILES)]
        v_grouped, v_mx, sums = {}, {}, {}

        def pick_values(j):
            window = val_pool[j][:].indirect(token_list[:])
            if j < SCALAR_PICKS:
                nc.scalar.activation(picked_vals[j][:], window, ACT.Copy)
            else:
                nc.vector.tensor_copy(picked_vals[j][:], window)

        def turn_values(j):
            pairs = picked_vals[j][:].bitcast(F32)
            turned = ps.tile([P, 2, P], F32, name=f"turned{j}", tag=bank_tags[j])
            for u in range(2):
                nc.tensor.transpose(turned[:, u, :], pairs[:, u::2], identity[:])
            v_grouped[j] = sb.tile([P, P * PACK], BF16, name=f"v_grouped{j}", tag=f"v_grouped{j}", align_bytes=ALIGN)
            nc.scalar.copy(
                v_grouped[j][:].bitcast(F32).rearrange("p (e u) -> p e u", u=2), turned[:].rearrange("p u e -> p e u")
            )

        def quantise_values(j):
            if j == LAST:
                tag = "member_pool0"
            else:
                tag = f"val_pool{j + 1}" if j + 1 >= SCALAR_PICKS else ""
            v_mx[j] = quantise(f"v{j}", v_grouped[j][:], P, tag)

        def add_up(j):
            acc = ps.tile([P, Q], F32, name=f"acc{j}", tag=bank_tags[j + 1])
            mx(acc[:], v_mx[j], slice(0, P), w_mx, slice(0, Q), True, True)
            sums[j] = sb.tile([P, Q], F32, name=f"sums{j}")
            nc.scalar.copy(sums[j][:], acc[:])

        def distance(j):
            second = j == 1
            diff = sb.tile([P, Q], F32, name=f"diff{j}", tag=f"v_grouped{LAST}" if second else "", align_bytes=ALIGN)
            dist = sb.tile([P, Q], F32, name=f"dist{j}", tag="member_pool0" if second else "", align_bytes=ALIGN)
            width = Q // 2 if j == LAST else Q
            for q0 in range(0, Q, width):
                cols = slice(q0, q0 + width)
                entries = member_list[:, q0 // PER_COLUMN : (q0 + width) // PER_COLUMN]
                nc.vector.tensor_tensor(
                    diff[:, cols], member_pool[j][:].indirect(entries), sums[j][:, cols], ALU.subtract
                )
                nc.scalar.activation(dist[:, cols], diff[:, cols], ACT.Abs)
                nc.sync.dma_start(out=out[j * P : (j + 1) * P, cols], in_=dist[:, cols])

        pick_values(0)
        for h in range(Q // P):
            nc.vector.scalar_tensor_tensor(
                out=w_grouped[:, h * P : (h + 1) * P, :],
                in0=score_banks[h][:].rearrange("p r q -> p q r"),
                scalar=0.0,
                in1=factor[:].unsqueeze(1).to_broadcast([P, P, PACK]),
                op0=ALU.max,
                op1=ALU.mult,
            )
        turn_values(0)
        w_mx = quantise("w", w_grouped[:].rearrange("p q r -> p (q r)"), Q)
        for j in range(1, E_TILES):
            pick_values(j)
            quantise_values(j - 1)
            turn_values(j)
            add_up(j - 1)
        distance(0)
        quantise_values(LAST)
        add_up(LAST)
        for j in range(1, E_TILES):
            distance(j)
